import numpy as np
import ml_dtypes


def mxq(x, axis, fmt="e4m3"):
    dtype, down = {"e4m3": (ml_dtypes.float8_e4m3fn, 7), "e5m2": (ml_dtypes.float8_e5m2, 14)}[fmt]
    v = np.moveaxis(np.asarray(x, np.float32).astype(ml_dtypes.bfloat16).astype(np.float64), axis, -1)
    blocks = v.reshape(v.shape[:-1] + (-1, 32))
    amax = np.abs(blocks).max(-1, keepdims=True)
    byte = np.maximum(np.where(amax > 0, np.frexp(amax)[1] - 1 + 127, 0) - down, 1)
    scale = np.exp2(byte - 127.0)
    codes = (blocks / scale).astype(np.float32).astype(dtype).astype(np.float64)
    return np.moveaxis((codes * scale).reshape(v.shape), -1, axis)


WIDE = False


def mx_kscale(k):
    if not WIDE:
        return np.ones(k)
    levels = np.array([10, -10, 5, -5, 0])
    if k % 512:
        return np.exp2(np.random.permutation(np.resize(levels, k // 32))).repeat(32)
    a = np.empty((k // 512, 16))
    for p in range(k // 512):
        a[p, :8] = np.random.permutation(np.resize(levels, 8))
        for g in range(8):
            far = levels[np.abs(levels - a[p, g]) >= 10]
            a[p, g + 8] = far[np.random.randint(len(far))]
    return np.exp2(a.ravel()).repeat(32)


def f64(x):
    return np.asarray(x).astype(np.float64)


def striped(idx):
    return np.tile(idx.reshape(-1, 16).T, (8, 1)).astype(np.uint16)


def unstriped(offs):
    return offs[:16].T.reshape(-1).astype(np.int64)


E2M1 = np.array([0.0, 0.5, 1.0, 1.5, 2.0, 3.0, 4.0, 6.0, -0.0, -0.5, -1.0, -1.5, -2.0, -3.0, -4.0, -6.0])


def pack_weight(w, fmt):
    k, n = w.shape
    w = f64(np.asarray(w, np.float32).astype(ml_dtypes.bfloat16)).reshape(k // 32, 32, n)
    amax = np.abs(w).max(1)
    if fmt == "e4m3":
        byte = np.frexp(amax)[1] - 1 + 127 - 7
    else:
        mant, ex = np.frexp(amax / 6.0)
        byte = np.where(mant > 0.5, ex, ex - 1) + 127
    byte = np.clip(np.where(amax > 0, byte, 1), 1, 254)
    scaled = (w * np.exp2(127.0 - byte)[:, None, :]).reshape(k, n).astype(np.float32)
    by_word = np.ascontiguousarray(scaled.reshape(k // 512, 128, 4, n).transpose(0, 1, 3, 2))
    if fmt == "e4m3":
        words = by_word.astype(ml_dtypes.float8_e4m3fn).view(np.uint8)
    else:
        c = by_word.astype(ml_dtypes.float4_e2m1fn).view(np.uint8) & 0xF
        words = (c[..., 0::2] | (c[..., 1::2] << 4)).reshape(k // 512, 128, 2 * n)
    return np.ascontiguousarray(words), np.ascontiguousarray(byte.astype(np.uint8).reshape(k // 512, 16, n))


def unpack_weight(words, scales, fmt):
    g, _, n = scales.shape
    words = np.ascontiguousarray(words).reshape(g, 128, n, -1)
    if fmt == "e4m3":
        vals = words.view(ml_dtypes.float8_e4m3fn).astype(np.float64)
    else:
        nib = np.empty((g, 128, n, 4), np.uint8)
        nib[..., 0::2] = words & 0xF
        nib[..., 1::2] = words >> 4
        vals = E2M1[nib]
    vals = vals * np.repeat(np.exp2(scales.astype(np.float64) - 127.0), 8, axis=1)[..., None]
    return vals.transpose(0, 1, 3, 2).reshape(g * 512, n)


def gelu(v):
    return 0.5 * v * (1.0 + np.tanh(np.sqrt(2.0 / np.pi) * (v + 0.044715 * v**3)))


K, T, S, P, P2, H, N = 1024, 4096, 1024, 512, 256, 512, 768

def setup_inputs():
    n = np.random.standard_normal
    s = mx_kscale(K)[:, None]
    u = mx_kscale(H)[:, None]
    tab_words, tab_scales = pack_weight(n((K, T)) * s, "e4m3")
    w1 = (n((K, H)) / np.sqrt(K) / s * u.T).astype(np.float32)
    w2_words, w2_scales = pack_weight(n((K, H)) / np.sqrt(K) / s * u.T, "e2m1")
    w3 = (n((K, H)) / np.sqrt(K) / s * u.T).astype(np.float32)
    w4_words, w4_scales = pack_weight(n((H, N)) / np.sqrt(H) / u, "e2m1")
    gam = (1.2 * np.exp(0.3 * n(H)) / u[:, 0]).astype(np.float32)
    gm = n((H, P2)).astype(np.float32)
    return {"tab_words": tab_words, "tab_scales": tab_scales,
            "offs": striped(np.random.permutation(T)[:S]),
            "pos1": striped(np.random.permutation(S)[:P]),
            "pos2": striped(np.random.permutation(S)[:P]),
            "pos3": striped(np.random.permutation(P)[:P2]),
            "pos4": striped(np.random.permutation(S)[:P2]),
            "w1": w1, "w2_words": w2_words, "w2_scales": w2_scales, "w3": w3,
            "w4_words": w4_words, "w4_scales": w4_scales, "gam": gam, "gm": gm}

def reference(tab_words, tab_scales, offs, pos1, pos2, pos3, pos4, w1, w2_words, w2_scales, w3,
              w4_words, w4_scales, gam, gm):
    v = unpack_weight(tab_words, tab_scales, "e4m3")[:, unstriped(offs)]
    w1q = mxq(f64(w1), 0, "e4m3")
    w2 = unpack_weight(w2_words, w2_scales, "e2m1")
    w3q = mxq(f64(w3), 0, "e4m3")
    w4 = unpack_weight(w4_words, w4_scales, "e2m1")
    h = np.maximum(w1q.T @ v, w2.T @ v) + (w3q.T @ v)
    a1 = h[:, unstriped(pos1)] * np.tanh(f64(gam)[:, None] * h[:, unstriped(pos2)])
    a2 = a1[:, unstriped(pos3)] * f64(gm) + h[:, unstriped(pos4)]
    a2q = mxq(a2, 0, "e4m3")
    return w4.T @ a2q

@@ -1,0 +1,241 @@
+from contextlib import ExitStack
+
+import concourse.mybir as mybir
+
+K, T, S, PAIRS, KEPT, H, N = 1024, 4096, 1024, 512, 256, 512, 768
+FLOPS = 2 * 3 * K * H * S + 2 * H * N * KEPT
+
+F32 = mybir.dt.float32
+BF16 = mybir.dt.bfloat16
+I32 = mybir.dt.int32
+U32 = mybir.dt.uint32
+U16 = mybir.dt.uint16
+U8 = mybir.dt.uint8
+E4M3X4 = mybir.dt.float8_e4m3fn_x4
+E2M1X4 = mybir.dt.float4_e2m1fn_x4
+ALU = mybir.AluOpType
+ACT = mybir.ActivationFunctionType
+
+P = 128
+PACK = 4
+K_PASS = P * PACK
+PASSES = K // K_PASS
+BANK = 512
+HALVES = S // BANK
+QUADS = 4
+QUAD = 32
+
+
+def tile_list_charter_dating_scores_kernel(
+    tc, tab_words, tab_scales, offs, pos1, pos2, pos3, pos4, w1, w2_words, w2_scales, w3,
+    w4_words, w4_scales, gam, gm, out,
+):
+    nc = tc.nc
+    with ExitStack() as ctx:
+        keep = ctx.enter_context(tc.tile_pool(name="keep", bufs=1))
+        psum = ctx.enter_context(tc.psum_pool(name="psum", bufs=8))
+
+        def sb(name, shape, dtype):
+            return keep.tile(shape, dtype, name=name, align_bytes=64)
+
+        def load_list(name, src):
+            tile = keep.tile(list(src.shape), U16, name=name)
+            nc.sync.dma_start(tile[:], src)
+            return tile
+
+        tab_s = sb("tab_s", [P, PASSES, T], U8)
+        w2s_raw = sb("w2s_raw", [P, PASSES, H], U8)
+        w4_s = sb("w4_s", [P, N], U8)
+        nc.vector.memset(tab_s[:, 0, :].bitcast(I32), 0)
+        nc.gpsimd.memset(tab_s[:, 1, :].bitcast(I32), 0)
+        nc.vector.memset(w2s_raw[:].rearrange("p a c -> p (a c)").bitcast(I32), 0)
+        nc.vector.memset(w4_s[:].bitcast(I32), 0)
+
+        offs_t = load_list("offs_t", offs)
+        tab_w = [sb(f"tab_w{a}", [P, T], U32) for a in range(PASSES)]
+        w2w_raw = sb("w2w_raw", [P, PASSES, 2 * H], U8)
+
+        def load_table(a, pieces):
+            words = tab_words[a].rearrange("p t i -> p (t i)").bitcast(I32)
+            step = T // pieces
+            for i in range(pieces):
+                nc.sync.dma_start(tab_w[a][:, i * step : (i + 1) * step].bitcast(I32), words[:, i * step : (i + 1) * step])
+
+        load_table(0, 4)
+        for q in range(QUADS):
+            nc.sync.dma_start(
+                tab_s[QUAD * q : QUAD * q + 4, :, :].bitcast(I32),
+                tab_scales[:, 4 * q : 4 * q + 4, :].rearrange("a r c -> r a c").bitcast(I32),
+            )
+        nc.sync.dma_start(w2w_raw[:].bitcast(I32), w2_words.rearrange("a p c -> p a c").bitcast(I32))
+        for q in range(QUADS):
+            nc.sync.dma_start(
+                w2s_raw[QUAD * q : QUAD * q + 4, :, :].bitcast(I32),
+                w2_scales[:, 4 * q : 4 * q + 4, :].rearrange("a r c -> r a c").bitcast(I32),
+            )
+        load_table(1, 2)
+        raw = {}
+        for name, w in (("w1", w1), ("w3", w3)):
+            for a in range(PASSES):
+                raw[name, a] = sb(f"{name}_raw{a}", [P, PACK, H], F32)
+                nc.sync.dma_start(
+                    raw[name, a][:], w[a * K_PASS : (a + 1) * K_PASS, :].rearrange("(p j) c -> p j c", j=PACK)
+                )
+        pos2_t = load_list("pos2_t", pos2)
+        gam_t = sb("gam_t", [P, PACK], F32)
+        nc.sync.dma_start(gam_t[:], gam.rearrange("(p t) -> p t", t=PACK))
+        pos1_t = load_list("pos1_t", pos1)
+        gm_t = sb("gm_t", [P, PACK, KEPT], F32)
+        nc.sync.dma_start(gm_t[:], gm.rearrange("(p t) j -> p t j", t=PACK))
+        pos3_t = load_list("pos3_t", pos3)
+        pos4_t = load_list("pos4_t", pos4)
+        w4_w = sb("w4_w", [P, 2 * N], U8)
+        nc.sync.dma_start(w4_w[:].bitcast(I32), w4_words[0].bitcast(I32))
+
+        for q in range(QUADS):
+            nc.sync.dma_start(
+                w4_s[QUAD * q : QUAD * q + 4, :].bitcast(I32), w4_scales[0, 4 * q : 4 * q + 4, :].bitcast(I32)
+            )
+
+        v_s = [sb(f"v_s{a}", [P, S], U8) for a in range(PASSES)]
+        v_w = {}
+
+        def gather_words(a):
+            cols = BANK // 16
+            for hf in range(HALVES):
+                v_w[a, hf] = sb(f"v_w{a}{hf}", [P, BANK], U32)
+                nc.vector.tensor_copy(v_w[a, hf][:], tab_w[a][:].indirect(offs_t[:, hf * cols : (hf + 1) * cols]))
+
+        gather_words(0)
+        for a in range(PASSES):
+            nc.vector.tensor_copy(v_s[a][:], tab_s[:, a, :].indirect(offs_t[:]))
+
+        w2_w = sb("w2_w", [P, PASSES, 2 * H], U8)
+        w2_s = sb("w2_s", [P, PASSES, H], U8)
+        nc.scalar.copy(
+            w2_w[:].bitcast(U16).rearrange("p a (t m) -> p a t m", t=PACK),
+            w2w_raw[:].bitcast(U16).rearrange("p a (m t) -> p a t m", t=PACK),
+        )
+        nc.vector.tensor_copy(
+            w2_s[:].rearrange("p a (t m) -> p a t m", t=PACK),
+            w2s_raw[:].rearrange("p a (m t) -> p a t m", t=PACK),
+        )
+        gather_words(1)
+
+        def product(acc, a, hf, lhsT, lhsT_scale):
+            nc.tensor.matmul_mx(
+                out=acc[:], lhsT=lhsT, lhsT_scale=lhsT_scale,
+                rhs=v_w[a, hf][:].bitcast(E4M3X4), rhs_scale=v_s[a][:, hf * BANK : (hf + 1) * BANK],
+                start=(a == 0), stop=(a == PASSES - 1),
+            )
+
+        second = [sb(f"second{t}", [P, S], F32) for t in range(PACK)]
+        accs = {}
+        for a in range(PASSES):
+            for hf in range(HALVES):
+                for t in range(PACK):
+                    if a == 0:
+                        accs[t, hf] = psum.tile([P, BANK], F32, name="acc")
+                    product(accs[t, hf], a, hf, w2_w[:, a, 2 * P * t : 2 * P * (t + 1)].bitcast(E2M1X4),
+                            w2_s[:, a, P * t : P * (t + 1)])
+                    if a == PASSES - 1:
+                        nc.scalar.copy(second[t][:, hf * BANK : (hf + 1) * BANK], accs[t, hf][:])
+
+        codes, scales = {}, {}
+
+        def round_weight(name, a, copies):
+            rounded = sb(f"{name}_bf{a}", [P, PACK * H], BF16)
+            dst = rounded[:].rearrange("p (t m j) -> p m j t", t=PACK, j=PACK)
+            src = raw[name, a][:].rearrange("p j (m t) -> p m j t", t=PACK)
+            step = P // len(copies)
+            for i, copy in enumerate(copies):
+                copy(dst[:, i * step : (i + 1) * step], src[:, i * step : (i + 1) * step])
+            return rounded
+
+        def quantise_weight(name, a, rounded):
+            codes[name, a] = sb(f"{name}_c{a}", [P, H], U32)
+            scales[name, a] = sb(f"{name}_s{a}", [P, H], U8)
+            nc.vector.quantize_mx(out=codes[name, a][:].bitcast(E4M3X4), scales=scales[name, a][:], in_=rounded[:])
+
+        def float_product(name, t, hf):
+            acc = psum.tile([P, BANK], F32, name="acc")
+            for a in range(PASSES):
+                product(acc, a, hf, codes[name, a][:, P * t : P * (t + 1)].bitcast(E4M3X4),
+                        scales[name, a][:, P * t : P * (t + 1)])
+            return acc
+
+        for a in range(PASSES):
+            quantise_weight("w1", a, round_weight("w1", a, [nc.vector.tensor_copy]))
+        w3_bf0 = round_weight("w3", 0, [nc.scalar.copy])
+        w3_bf1 = round_weight("w3", 1, [nc.scalar.copy, nc.vector.tensor_copy])
+
+        larger = [sb(f"larger{t}", [P, S], F32) for t in range(PACK)]
+        for t in range(PACK):
+            for hf in range(HALVES):
+                cols = slice(hf * BANK, (hf + 1) * BANK)
+                acc = float_product("w1", t, hf)
+                nc.vector.tensor_tensor(larger[t][:, cols], acc[:], second[t][:, cols], ALU.max)
+            if t == 1:
+                quantise_weight("w3", 0, w3_bf0)
+            if t == 2:
+                quantise_weight("w3", 1, w3_bf1)
+
+        h = [sb(f"h{t}", [P, S], F32) for t in range(PACK)]
+        picked = [sb(f"picked{t}", [P, PAIRS], F32) for t in range(PACK)]
+        gate = [sb(f"gate{t}", [P, PAIRS], F32) for t in range(PACK)]
+        a1 = [sb(f"a1_{t}", [P, PAIRS], F32) for t in range(PACK)]
+        kept = [sb(f"kept{t}", [P, KEPT], F32) for t in range(PACK)]
+        a2 = sb("a2", [P, PACK, KEPT], F32)
+
+        def features(t):
+            for hf in range(HALVES):
+                cols = slice(hf * BANK, (hf + 1) * BANK)
+                acc = float_product("w3", t, hf)
+                nc.vector.tensor_tensor(h[t][:, cols], acc[:], larger[t][:, cols], ALU.add)
+
+        def pick_second(t):
+            nc.vector.tensor_copy(picked[t][:], h[t][:].indirect(pos2_t[:]))
+            nc.scalar.activation(gate[t][:], picked[t][:], ACT.Tanh, scale=gam_t[:, t : t + 1])
+
+        def pair(t):
+            nc.vector.tensor_tensor(a1[t][:], h[t][:].indirect(pos1_t[:]), gate[t][:], ALU.mult)
+
+        def keep_pairs(t):
+            nc.vector.tensor_tensor(kept[t][:], a1[t][:].indirect(pos3_t[:]), gm_t[:, t, :], ALU.mult)
+
+        def add_deed(t):
+            nc.vector.tensor_tensor(a2[:, t, :], h[t][:].indirect(pos4_t[:]), kept[t][:], ALU.add)
+
+        features(0)
+        pick_second(0)
+        for t in range(PACK):
+            if t + 1 < PACK:
+                features(t + 1)
+            pair(t)
+            if t + 1 < PACK:
+                pick_second(t + 1)
+            keep_pairs(t)
+            if t > 0:
+                add_deed(t - 1)
+        add_deed(PACK - 1)
+
+        a2_bf = sb("a2_bf", [P, KEPT * PACK], BF16)
+        nc.vector.tensor_copy(
+            a2_bf[:].rearrange("p (c i t) -> p c t i", i=4, t=PACK),
+            a2[:].rearrange("p t (c i) -> p c t i", i=4),
+        )
+        a2_c = sb("a2_c", [P, KEPT], U32)
+        a2_s = sb("a2_s", [P, KEPT], U8)
+        nc.vector.quantize_mx(out=a2_c[:].bitcast(E4M3X4), scales=a2_s[:], in_=a2_bf[:])
+
+        for c in range(N // P):
+            acc = psum.tile([P, KEPT], F32, name="acc")
+            nc.tensor.matmul_mx(
+                out=acc[:], lhsT=w4_w[:, 2 * P * c : 2 * P * (c + 1)].bitcast(E2M1X4),
+                lhsT_scale=w4_s[:, P * c : P * (c + 1)],
+                rhs=a2_c[:].bitcast(E4M3X4), rhs_scale=a2_s[:], start=True, stop=True,
+            )
+            scores = sb(f"scores{c}", [P, KEPT], F32)
+            copy = nc.scalar.copy if c % 2 == 0 else nc.vector.tensor_copy
+            copy(scores[:], acc[:])
+            nc.sync.dma_start(out[P * c : P * (c + 1), :], scores[:])

@@ -51,17 +51,22 @@ def tile_list_charter_dating_scores_kernel(
         nc.vector.memset(w2s_raw[:].rearrange("p a c -> p (a c)").bitcast(I32), 0)
         nc.vector.memset(w4_s[:].bitcast(I32), 0)
 
-        offs_t = load_list("offs_t", offs)
         tab_w = [sb(f"tab_w{a}", [P, T], U32) for a in range(PASSES)]
         w2w_raw = sb("w2w_raw", [P, PASSES, 2 * H], U8)
 
-        def load_table(a, pieces):
+        def load_table(a, cols):
             words = tab_words[a].rearrange("p t i -> p (t i)").bitcast(I32)
-            step = T // pieces
-            for i in range(pieces):
-                nc.sync.dma_start(tab_w[a][:, i * step : (i + 1) * step].bitcast(I32), words[:, i * step : (i + 1) * step])
+            nc.sync.dma_start(tab_w[a][:, cols].bitcast(I32), words[:, cols])
 
-        load_table(0, 4)
+        load_table(0, slice(0, T // 2))
+        offs_t = load_list("offs_t", offs)
+        pos2_t = load_list("pos2_t", pos2)
+        pos1_t = load_list("pos1_t", pos1)
+        pos3_t = load_list("pos3_t", pos3)
+        pos4_t = load_list("pos4_t", pos4)
+        gam_t = sb("gam_t", [P, PACK], F32)
+        nc.sync.dma_start(gam_t[:], gam.rearrange("(p t) -> p t", t=PACK))
+        load_table(0, slice(T // 2, T))
         for q in range(QUADS):
             nc.sync.dma_start(
                 tab_s[QUAD * q : QUAD * q + 4, :, :].bitcast(I32),
@@ -73,22 +78,20 @@ def tile_list_charter_dating_scores_kernel(
                 w2s_raw[QUAD * q : QUAD * q + 4, :, :].bitcast(I32),
                 w2_scales[:, 4 * q : 4 * q + 4, :].rearrange("a r c -> r a c").bitcast(I32),
             )
-        load_table(1, 2)
+        load_table(1, slice(0, T))
         raw = {}
         for name, w in (("w1", w1), ("w3", w3)):
             for a in range(PASSES):
-                raw[name, a] = sb(f"{name}_raw{a}", [P, PACK, H], F32)
-                nc.sync.dma_start(
-                    raw[name, a][:], w[a * K_PASS : (a + 1) * K_PASS, :].rearrange("(p j) c -> p j c", j=PACK)
-                )
-        pos2_t = load_list("pos2_t", pos2)
-        gam_t = sb("gam_t", [P, PACK], F32)
-        nc.sync.dma_start(gam_t[:], gam.rearrange("(p t) -> p t", t=PACK))
-        pos1_t = load_list("pos1_t", pos1)
+                rows = w[a * K_PASS : (a + 1) * K_PASS, :].rearrange("(p j) c -> p j c", j=PACK)
+                pieces = 2 if (name, a) == ("w3", 1) else 1
+                step = H // pieces
+                raw[name, a] = []
+                for i in range(pieces):
+                    piece = sb(f"{name}_raw{a}{i}", [P, PACK, step], F32)
+                    nc.sync.dma_start(piece[:], rows[:, :, i * step : (i + 1) * step])
+                    raw[name, a].append(piece)
         gm_t = sb("gm_t", [P, PACK, KEPT], F32)
         nc.sync.dma_start(gm_t[:], gm.rearrange("(p t) j -> p t j", t=PACK))
-        pos3_t = load_list("pos3_t", pos3)
-        pos4_t = load_list("pos4_t", pos4)
         w4_w = sb("w4_w", [P, 2 * N], U8)
         nc.sync.dma_start(w4_w[:].bitcast(I32), w4_words[0].bitcast(I32))
 
@@ -145,11 +148,10 @@ def tile_list_charter_dating_scores_kernel(
 
         def round_weight(name, a, copies):
             rounded = sb(f"{name}_bf{a}", [P, PACK * H], BF16)
-            dst = rounded[:].rearrange("p (t m j) -> p m j t", t=PACK, j=PACK)
-            src = raw[name, a][:].rearrange("p j (m t) -> p m j t", t=PACK)
+            dst = rounded[:].rearrange("p (t m j) -> p m t j", t=PACK, j=PACK)
             step = P // len(copies)
-            for i, copy in enumerate(copies):
-                copy(dst[:, i * step : (i + 1) * step], src[:, i * step : (i + 1) * step])
+            for i, (piece, copy) in enumerate(zip(raw[name, a], copies)):
+                copy(dst[:, i * step : (i + 1) * step], piece[:].rearrange("p j (m t) -> p m t j", t=PACK))
             return rounded
 
         def quantise_weight(name, a, rounded):
@@ -166,8 +168,8 @@ def tile_list_charter_dating_scores_kernel(
 
         for a in range(PASSES):
             quantise_weight("w1", a, round_weight("w1", a, [nc.vector.tensor_copy]))
-        w3_bf0 = round_weight("w3", 0, [nc.scalar.copy])
-        w3_bf1 = round_weight("w3", 1, [nc.scalar.copy, nc.vector.tensor_copy])
+        quantise_weight("w3", 0, round_weight("w3", 0, [nc.scalar.copy]))
+        quantise_weight("w3", 1, round_weight("w3", 1, [nc.vector.tensor_copy, nc.scalar.copy]))
 
         larger = [sb(f"larger{t}", [P, S], F32) for t in range(PACK)]
         for t in range(PACK):
@@ -175,10 +177,6 @@ def tile_list_charter_dating_scores_kernel(
                 cols = slice(hf * BANK, (hf + 1) * BANK)
                 acc = float_product("w1", t, hf)
                 nc.vector.tensor_tensor(larger[t][:, cols], acc[:], second[t][:, cols], ALU.max)
-            if t == 1:
-                quantise_weight("w3", 0, w3_bf0)
-            if t == 2:
-                quantise_weight("w3", 1, w3_bf1)
 
         h = [sb(f"h{t}", [P, S], F32) for t in range(PACK)]
         picked = [sb(f"picked{t}", [P, PAIRS], F32) for t in range(PACK)]

@@ -67,16 +67,16 @@ def tile_list_charter_dating_scores_kernel(
         gam_t = sb("gam_t", [P, PACK], F32)
         nc.sync.dma_start(gam_t[:], gam.rearrange("(p t) -> p t", t=PACK))
         load_table(0, slice(T // 2, T))
-        for q in range(QUADS):
+        for r in range(4):
             nc.sync.dma_start(
-                tab_s[QUAD * q : QUAD * q + 4, :, :].bitcast(I32),
-                tab_scales[:, 4 * q : 4 * q + 4, :].rearrange("a r c -> r a c").bitcast(I32),
+                tab_s[r:P:QUAD, :, :].bitcast(I32),
+                tab_scales[:, r:16:4, :].rearrange("a q c -> q a c").bitcast(I32),
             )
         nc.sync.dma_start(w2w_raw[:].bitcast(I32), w2_words.rearrange("a p c -> p a c").bitcast(I32))
-        for q in range(QUADS):
+        for r in range(4):
             nc.sync.dma_start(
-                w2s_raw[QUAD * q : QUAD * q + 4, :, :].bitcast(I32),
-                w2_scales[:, 4 * q : 4 * q + 4, :].rearrange("a r c -> r a c").bitcast(I32),
+                w2s_raw[r:P:QUAD, :, :].bitcast(I32),
+                w2_scales[:, r:16:4, :].rearrange("a q c -> q a c").bitcast(I32),
             )
         load_table(1, slice(0, T))
         raw = {}
@@ -95,10 +95,8 @@ def tile_list_charter_dating_scores_kernel(
         w4_w = sb("w4_w", [P, 2 * N], U8)
         nc.sync.dma_start(w4_w[:].bitcast(I32), w4_words[0].bitcast(I32))
 
-        for q in range(QUADS):
-            nc.sync.dma_start(
-                w4_s[QUAD * q : QUAD * q + 4, :].bitcast(I32), w4_scales[0, 4 * q : 4 * q + 4, :].bitcast(I32)
-            )
+        for r in range(4):
+            nc.sync.dma_start(w4_s[r:P:QUAD, :].bitcast(I32), w4_scales[0, r:16:4, :].bitcast(I32))
 
         v_s = [sb(f"v_s{a}", [P, S], U8) for a in range(PASSES)]
         v_w = {}

@@ -1,6 +1,7 @@
 from contextlib import ExitStack
 
 import concourse.mybir as mybir
+from concourse.masks import make_identity
 
 K, T, S, PAIRS, KEPT, H, N = 1024, 4096, 1024, 512, 256, 512, 768
 FLOPS = 2 * 3 * K * H * S + 2 * H * N * KEPT
@@ -22,8 +23,19 @@ K_PASS = P * PACK
 PASSES = K // K_PASS
 BANK = 512
 HALVES = S // BANK
-QUADS = 4
+BLOCKS = BANK // P
+PART = KEPT // 2
 QUAD = 32
+ROWS = 4
+ENTRIES = 16
+DIRECT = 2
+SUM_BANKS, TURN_BANKS = 6, 2
+
+AT_TAB_W1 = 0
+AT_W3 = (0, 8)
+AT_W1 = (16, 24)
+AT_TAB_S = 22
+AT_GM, AT_W4_W, AT_W4_S = 24, 28, 30
 
 
 def tile_list_charter_dating_scores_kernel(
@@ -33,32 +45,38 @@ def tile_list_charter_dating_scores_kernel(
     nc = tc.nc
     with ExitStack() as ctx:
         keep = ctx.enter_context(tc.tile_pool(name="keep", bufs=1))
-        psum = ctx.enter_context(tc.psum_pool(name="psum", bufs=8))
+        reuse = ctx.enter_context(tc.tile_pool(name="reuse", bufs=1))
+        psum = ctx.enter_context(tc.psum_pool(name="psum", bufs=SUM_BANKS))
 
         def sb(name, shape, dtype):
             return keep.tile(shape, dtype, name=name, align_bytes=64)
+
+        def shared(name, shape, dtype, kib):
+            return reuse.tile(shape, dtype, name=name, align_bytes=64, offset=kib * 1024)
 
         def load_list(name, src):
             tile = keep.tile(list(src.shape), U16, name=name)
             nc.sync.dma_start(tile[:], src)
             return tile
 
-        tab_s = sb("tab_s", [P, PASSES, T], U8)
+        tab_s = shared("tab_s", [P, T], U8, AT_TAB_S)
         w2s_raw = sb("w2s_raw", [P, PASSES, H], U8)
-        w4_s = sb("w4_s", [P, N], U8)
-        nc.vector.memset(tab_s[:, 0, :].bitcast(I32), 0)
-        nc.gpsimd.memset(tab_s[:, 1, :].bitcast(I32), 0)
+        v_s = [sb(f"v_s{a}", [P, S], U8) for a in range(PASSES)]
+        nc.vector.memset(tab_s[:, : T // 2].bitcast(I32), 0)
+        nc.gpsimd.memset(tab_s[:, T // 2 :].bitcast(I32), 0)
         nc.vector.memset(w2s_raw[:].rearrange("p a c -> p (a c)").bitcast(I32), 0)
-        nc.vector.memset(w4_s[:].bitcast(I32), 0)
+        nc.vector.memset(v_s[1][:].bitcast(I32), 0)
+        ident = sb("ident", [P, P], F32)
+        make_identity(nc, ident[:])
 
-        tab_w = [sb(f"tab_w{a}", [P, T], U32) for a in range(PASSES)]
+        tab_w = [sb("tab_w0", [P, T], U32), shared("tab_w1", [P, T], U32, AT_TAB_W1)]
         w2w_raw = sb("w2w_raw", [P, PASSES, 2 * H], U8)
 
         def load_table(a, cols):
             words = tab_words[a].rearrange("p t i -> p (t i)").bitcast(I32)
             nc.sync.dma_start(tab_w[a][:, cols].bitcast(I32), words[:, cols])
 
-        load_table(0, slice(0, T // 2))
+        load_table(0, slice(0, T // 4))
         offs_t = load_list("offs_t", offs)
         pos2_t = load_list("pos2_t", pos2)
         pos1_t = load_list("pos1_t", pos1)
@@ -66,50 +84,43 @@ def tile_list_charter_dating_scores_kernel(
         pos4_t = load_list("pos4_t", pos4)
         gam_t = sb("gam_t", [P, PACK], F32)
         nc.sync.dma_start(gam_t[:], gam.rearrange("(p t) -> p t", t=PACK))
-        load_table(0, slice(T // 2, T))
-        for r in range(4):
+        load_table(0, slice(T // 4, 5 * T // 8))
+        for r in range(ROWS):
             nc.sync.dma_start(
-                tab_s[r:P:QUAD, :, :].bitcast(I32),
-                tab_scales[:, r:16:4, :].rearrange("a q c -> q a c").bitcast(I32),
+                tab_s[r : P : QUAD // PASSES, :].bitcast(I32),
+                tab_scales[:, r : ROWS * ROWS : ROWS, :].rearrange("a q c -> q a c").bitcast(I32),
             )
+        load_table(0, slice(5 * T // 8, T))
         nc.sync.dma_start(w2w_raw[:].bitcast(I32), w2_words.rearrange("a p c -> p a c").bitcast(I32))
-        for r in range(4):
+        for r in range(ROWS):
             nc.sync.dma_start(
                 w2s_raw[r:P:QUAD, :, :].bitcast(I32),
-                w2_scales[:, r:16:4, :].rearrange("a q c -> q a c").bitcast(I32),
+                w2_scales[:, r : ROWS * ROWS : ROWS, :].rearrange("a q c -> q a c").bitcast(I32),
             )
         load_table(1, slice(0, T))
-        raw = {}
-        for name, w in (("w1", w1), ("w3", w3)):
-            for a in range(PASSES):
-                rows = w[a * K_PASS : (a + 1) * K_PASS, :].rearrange("(p j) c -> p j c", j=PACK)
-                pieces = 2 if (name, a) == ("w3", 1) else 1
-                step = H // pieces
-                raw[name, a] = []
-                for i in range(pieces):
-                    piece = sb(f"{name}_raw{a}{i}", [P, PACK, step], F32)
-                    nc.sync.dma_start(piece[:], rows[:, :, i * step : (i + 1) * step])
-                    raw[name, a].append(piece)
-        gm_t = sb("gm_t", [P, PACK, KEPT], F32)
-        nc.sync.dma_start(gm_t[:], gm.rearrange("(p t) j -> p t j", t=PACK))
-        w4_w = sb("w4_w", [P, 2 * N], U8)
-        nc.sync.dma_start(w4_w[:].bitcast(I32), w4_words[0].bitcast(I32))
 
-        for r in range(4):
-            nc.sync.dma_start(w4_s[r:P:QUAD, :].bitcast(I32), w4_scales[0, r:16:4, :].bitcast(I32))
-
-        v_s = [sb(f"v_s{a}", [P, S], U8) for a in range(PASSES)]
         v_w = {}
 
         def gather_words(a):
-            cols = BANK // 16
+            cols = BANK // ENTRIES
             for hf in range(HALVES):
                 v_w[a, hf] = sb(f"v_w{a}{hf}", [P, BANK], U32)
                 nc.vector.tensor_copy(v_w[a, hf][:], tab_w[a][:].indirect(offs_t[:, hf * cols : (hf + 1) * cols]))
 
-        gather_words(0)
+        raw = {}
+
+        def load_weight(name, w, a, kib):
+            raw[name, a] = shared(f"{name}_raw{a}", [P, PACK, H], F32, kib)
+            nc.sync.dma_start(
+                raw[name, a][:], w[a * K_PASS : (a + 1) * K_PASS, :].rearrange("(p j) c -> p j c", j=PACK)
+            )
+
+        nc.vector.tensor_copy(v_s[0][:], tab_s[:].indirect(offs_t[:]))
+        for r in range(ROWS):
+            nc.sync.dma_start(v_s[1][r:P:QUAD, :].bitcast(I32), v_s[0][QUAD // PASSES + r : P : QUAD, :].bitcast(I32))
         for a in range(PASSES):
-            nc.vector.tensor_copy(v_s[a][:], tab_s[:, a, :].indirect(offs_t[:]))
+            load_weight("w1", w1, a, AT_W1[a])
+        gather_words(0)
 
         w2_w = sb("w2_w", [P, PASSES, 2 * H], U8)
         w2_s = sb("w2_s", [P, PASSES, H], U8)
@@ -122,52 +133,74 @@ def tile_list_charter_dating_scores_kernel(
             w2s_raw[:].rearrange("p a (m t) -> p a t m", t=PACK),
         )
         gather_words(1)
+        for a in range(PASSES):
+            load_weight("w3", w3, a, AT_W3[a])
 
-        def product(acc, a, hf, lhsT, lhsT_scale):
-            nc.tensor.matmul_mx(
-                out=acc[:], lhsT=lhsT, lhsT_scale=lhsT_scale,
-                rhs=v_w[a, hf][:].bitcast(E4M3X4), rhs_scale=v_s[a][:, hf * BANK : (hf + 1) * BANK],
-                start=(a == 0), stop=(a == PASSES - 1),
-            )
+        def product(acc, a, t, hf, weight, weight_scale):
+            if t < DIRECT:
+                nc.tensor.matmul_mx(
+                    out=acc[:], lhsT=weight, lhsT_scale=weight_scale,
+                    rhs=v_w[a, hf][:].bitcast(E4M3X4), rhs_scale=v_s[a][:, hf * BANK : (hf + 1) * BANK],
+                    start=(a == 0), stop=(a == PASSES - 1),
+                )
+                return
+            for i in range(BLOCKS):
+                first = hf * BANK + P * i
+                nc.tensor.matmul_mx(
+                    out=acc[:, P * i : P * (i + 1)], lhsT=v_w[a, hf][:, P * i : P * (i + 1)].bitcast(E4M3X4),
+                    lhsT_scale=v_s[a][:, first : first + P], rhs=weight, rhs_scale=weight_scale,
+                    start=(a, i) == (0, 0), stop=(a, i) == (PASSES - 1, BLOCKS - 1),
+                )
 
         second = [sb(f"second{t}", [P, S], F32) for t in range(PACK)]
         accs = {}
-        for a in range(PASSES):
-            for hf in range(HALVES):
+        for hf in range(HALVES):
+            for a in range(PASSES):
                 for t in range(PACK):
                     if a == 0:
                         accs[t, hf] = psum.tile([P, BANK], F32, name="acc")
-                    product(accs[t, hf], a, hf, w2_w[:, a, 2 * P * t : 2 * P * (t + 1)].bitcast(E2M1X4),
+                    product(accs[t, hf], a, t, hf, w2_w[:, a, 2 * P * t : 2 * P * (t + 1)].bitcast(E2M1X4),
                             w2_s[:, a, P * t : P * (t + 1)])
                     if a == PASSES - 1:
                         nc.scalar.copy(second[t][:, hf * BANK : (hf + 1) * BANK], accs[t, hf][:])
 
         codes, scales = {}, {}
 
-        def round_weight(name, a, copies):
+        def quantise_weight(name, a, copy, pieces):
             rounded = sb(f"{name}_bf{a}", [P, PACK * H], BF16)
-            dst = rounded[:].rearrange("p (t m j) -> p m t j", t=PACK, j=PACK)
-            step = P // len(copies)
-            for i, (piece, copy) in enumerate(zip(raw[name, a], copies)):
-                copy(dst[:, i * step : (i + 1) * step], piece[:].rearrange("p j (m t) -> p m t j", t=PACK))
-            return rounded
-
-        def quantise_weight(name, a, rounded):
+            copy(
+                rounded[:].rearrange("p (t m j) -> p m t j", t=PACK, j=PACK),
+                raw[name, a][:].rearrange("p j (m t) -> p m t j", t=PACK),
+            )
             codes[name, a] = sb(f"{name}_c{a}", [P, H], U32)
             scales[name, a] = sb(f"{name}_s{a}", [P, H], U8)
-            nc.vector.quantize_mx(out=codes[name, a][:].bitcast(E4M3X4), scales=scales[name, a][:], in_=rounded[:])
+            step = H // pieces
+            for first in range(0, H, step):
+                nc.vector.quantize_mx(
+                    out=codes[name, a][:, first : first + step].bitcast(E4M3X4),
+                    scales=scales[name, a][:, first : first + step],
+                    in_=rounded[:, PACK * first : PACK * (first + step)],
+                )
 
         def float_product(name, t, hf):
             acc = psum.tile([P, BANK], F32, name="acc")
             for a in range(PASSES):
-                product(acc, a, hf, codes[name, a][:, P * t : P * (t + 1)].bitcast(E4M3X4),
+                product(acc, a, t, hf, codes[name, a][:, P * t : P * (t + 1)].bitcast(E4M3X4),
                         scales[name, a][:, P * t : P * (t + 1)])
             return acc
 
         for a in range(PASSES):
-            quantise_weight("w1", a, round_weight("w1", a, [nc.vector.tensor_copy]))
-        quantise_weight("w3", 0, round_weight("w3", 0, [nc.scalar.copy]))
-        quantise_weight("w3", 1, round_weight("w3", 1, [nc.vector.tensor_copy, nc.scalar.copy]))
+            quantise_weight("w1", a, nc.vector.tensor_copy, 1)
+        gm_t = shared("gm_t", [P, PACK, KEPT], F32, AT_GM)
+        nc.sync.dma_start(gm_t[:], gm.rearrange("(p t) j -> p t j", t=PACK))
+        w4_w = shared("w4_w", [P, 2 * N], U8, AT_W4_W)
+        nc.sync.dma_start(w4_w[:].bitcast(I32), w4_words[0].bitcast(I32))
+        w4_s = shared("w4_s", [P, N], U8, AT_W4_S)
+        nc.gpsimd.memset(w4_s[:].bitcast(I32), 0)
+        for r in range(ROWS):
+            nc.sync.dma_start(w4_s[r:P:QUAD, :].bitcast(I32), w4_scales[0, r : ROWS * ROWS : ROWS, :].bitcast(I32))
+        quantise_weight("w3", 0, nc.scalar.copy, 1)
+        quantise_weight("w3", 1, nc.scalar.copy, 2)
 
         larger = [sb(f"larger{t}", [P, S], F32) for t in range(PACK)]
         for t in range(PACK):
@@ -187,7 +220,19 @@ def tile_list_charter_dating_scores_kernel(
             for hf in range(HALVES):
                 cols = slice(hf * BANK, (hf + 1) * BANK)
                 acc = float_product("w3", t, hf)
-                nc.vector.tensor_tensor(h[t][:, cols], acc[:], larger[t][:, cols], ALU.add)
+                if t < DIRECT:
+                    nc.vector.tensor_tensor(h[t][:, cols], acc[:], larger[t][:, cols], ALU.add)
+                    continue
+                third = sb(f"third{t}{hf}", [P, BANK], F32)
+                nc.scalar.copy(third[:], acc[:])
+                turned = psum.tile([P, BANK], F32, name="turned", bufs=TURN_BANKS)
+                for n, term in enumerate((larger[t][:, cols], third[:])):
+                    for i in range(BLOCKS):
+                        nc.tensor.matmul(
+                            turned[:, P * i : P * (i + 1)], lhsT=term[:, P * i : P * (i + 1)], rhs=ident[:],
+                            is_transpose=True, start=(n, i) == (0, 0), stop=(n, i) == (1, BLOCKS - 1),
+                        )
+                nc.scalar.copy(h[t][:, cols], turned[:])
 
         def pick_second(t):
             nc.vector.tensor_copy(picked[t][:], h[t][:].indirect(pos2_t[:]))
@@ -196,42 +241,60 @@ def tile_list_charter_dating_scores_kernel(
         def pair(t):
             nc.vector.tensor_tensor(a1[t][:], h[t][:].indirect(pos1_t[:]), gate[t][:], ALU.mult)
 
-        def keep_pairs(t):
-            nc.vector.tensor_tensor(kept[t][:], a1[t][:].indirect(pos3_t[:]), gm_t[:, t, :], ALU.mult)
+        def keep_pairs(t, first, end):
+            entries = pos3_t[:, first // ENTRIES : end // ENTRIES]
+            nc.vector.tensor_tensor(kept[t][:, first:end], a1[t][:].indirect(entries), gm_t[:, t, first:end], ALU.mult)
 
-        def add_deed(t):
-            nc.vector.tensor_tensor(a2[:, t, :], h[t][:].indirect(pos4_t[:]), kept[t][:], ALU.add)
+        def add_deed(t, first, end):
+            entries = pos4_t[:, first // ENTRIES : end // ENTRIES]
+            nc.vector.tensor_tensor(a2[:, t, first:end], h[t][:].indirect(entries), kept[t][:, first:end], ALU.add)
 
         features(0)
         pick_second(0)
-        for t in range(PACK):
-            if t + 1 < PACK:
-                features(t + 1)
+        for t in range(1, PACK):
+            features(t)
+        last = PACK - 1
+        for t in range(last):
             pair(t)
-            if t + 1 < PACK:
-                pick_second(t + 1)
-            keep_pairs(t)
+            pick_second(t + 1)
+            keep_pairs(t, 0, KEPT)
             if t > 0:
-                add_deed(t - 1)
-        add_deed(PACK - 1)
+                add_deed(t - 1, 0, KEPT)
+        pair(last)
 
-        a2_bf = sb("a2_bf", [P, KEPT * PACK], BF16)
-        nc.vector.tensor_copy(
-            a2_bf[:].rearrange("p (c i t) -> p c t i", i=4, t=PACK),
-            a2[:].rearrange("p t (c i) -> p c t i", i=4),
-        )
-        a2_c = sb("a2_c", [P, KEPT], U32)
-        a2_s = sb("a2_s", [P, KEPT], U8)
-        nc.vector.quantize_mx(out=a2_c[:].bitcast(E4M3X4), scales=a2_s[:], in_=a2_bf[:])
+        a2_bf = [sb(f"a2_bf{u}", [P, PART * PACK], BF16) for u in range(KEPT // PART)]
 
-        for c in range(N // P):
-            acc = psum.tile([P, KEPT], F32, name="acc")
-            nc.tensor.matmul_mx(
-                out=acc[:], lhsT=w4_w[:, 2 * P * c : 2 * P * (c + 1)].bitcast(E2M1X4),
-                lhsT_scale=w4_s[:, P * c : P * (c + 1)],
-                rhs=a2_c[:].bitcast(E4M3X4), rhs_scale=a2_s[:], start=True, stop=True,
+        def round_a2(u):
+            nc.vector.tensor_copy(
+                a2_bf[u][:].rearrange("p (c i t) -> p c t i", i=4, t=PACK),
+                a2[:, :, PART * u : PART * (u + 1)].rearrange("p t (c i) -> p c t i", i=4),
             )
-            scores = sb(f"scores{c}", [P, KEPT], F32)
-            copy = nc.scalar.copy if c % 2 == 0 else nc.vector.tensor_copy
-            copy(scores[:], acc[:])
-            nc.sync.dma_start(out[P * c : P * (c + 1), :], scores[:])
+
+        def score(u, copies):
+            a2_c = sb(f"a2_c{u}", [P, PART], U32)
+            a2_s = sb(f"a2_s{u}", [P, PART], U8)
+            nc.vector.quantize_mx(out=a2_c[:].bitcast(E4M3X4), scales=a2_s[:], in_=a2_bf[u][:])
+            groups = N // P // len(copies)
+            for g, copy in enumerate(copies):
+                acc = psum.tile([P, groups, PART], F32, name="acc")
+                for i in range(groups):
+                    c = g * groups + i
+                    nc.tensor.matmul_mx(
+                        out=acc[:, i, :], lhsT=w4_w[:, 2 * P * c : 2 * P * (c + 1)].bitcast(E2M1X4),
+                        lhsT_scale=w4_s[:, P * c : P * (c + 1)],
+                        rhs=a2_c[:].bitcast(E4M3X4), rhs_scale=a2_s[:], start=True, stop=True,
+                    )
+                result = sb(f"result{u}{g}", [P, groups, PART], F32)
+                copy(result[:], acc[:])
+                rows = out[g * groups * P : (g + 1) * groups * P, PART * u : PART * (u + 1)]
+                nc.sync.dma_start(rows.rearrange("(i p) j -> p i j", p=P), result[:])
+
+        keep_pairs(last, 0, PART)
+        add_deed(last - 1, 0, KEPT)
+        add_deed(last, 0, PART)
+        keep_pairs(last, PART, KEPT)
+        round_a2(0)
+        add_deed(last, PART, KEPT)
+        score(0, [nc.scalar.copy, nc.scalar.copy])
+        round_a2(1)
+        score(1, [nc.scalar.copy, nc.vector.tensor_copy])

from contextlib import ExitStack

import concourse.mybir as mybir
from concourse.masks import make_identity

K, T, S, PAIRS, KEPT, H, N = 1024, 4096, 1024, 512, 256, 512, 768
FLOPS = 2 * 3 * K * H * S + 2 * H * N * KEPT

F32 = mybir.dt.float32
BF16 = mybir.dt.bfloat16
I32 = mybir.dt.int32
U32 = mybir.dt.uint32
U16 = mybir.dt.uint16
U8 = mybir.dt.uint8
E4M3X4 = mybir.dt.float8_e4m3fn_x4
E2M1X4 = mybir.dt.float4_e2m1fn_x4
ALU = mybir.AluOpType
ACT = mybir.ActivationFunctionType

P = 128
PACK = 4
K_PASS = P * PACK
PASSES = K // K_PASS
BANK = 512
HALVES = S // BANK
BLOCKS = BANK // P
PART = KEPT // 2
QUAD = 32
ROWS = 4
ENTRIES = 16
DIRECT = 2
SUM_BANKS, TURN_BANKS = 6, 2

AT_TAB_W1 = 0
AT_W3 = (0, 8)
AT_W1 = (16, 24)
AT_TAB_S = 22
AT_GM, AT_W4_W, AT_W4_S = 24, 28, 30


def tile_list_charter_dating_scores_kernel(
    tc, tab_words, tab_scales, offs, pos1, pos2, pos3, pos4, w1, w2_words, w2_scales, w3,
    w4_words, w4_scales, gam, gm, out,
):
    nc = tc.nc
    with ExitStack() as ctx:
        keep = ctx.enter_context(tc.tile_pool(name="keep", bufs=1))
        reuse = ctx.enter_context(tc.tile_pool(name="reuse", bufs=1))
        psum = ctx.enter_context(tc.psum_pool(name="psum", bufs=SUM_BANKS))

        def sb(name, shape, dtype):
            return keep.tile(shape, dtype, name=name, align_bytes=64)

        def shared(name, shape, dtype, kib):
            return reuse.tile(shape, dtype, name=name, align_bytes=64, offset=kib * 1024)

        def load_list(name, src):
            tile = keep.tile(list(src.shape), U16, name=name)
            nc.sync.dma_start(tile[:], src)
            return tile

        tab_s = shared("tab_s", [P, T], U8, AT_TAB_S)
        w2s_raw = sb("w2s_raw", [P, PASSES, H], U8)
        v_s = [sb(f"v_s{a}", [P, S], U8) for a in range(PASSES)]
        nc.vector.memset(tab_s[:, : T // 2].bitcast(I32), 0)
        nc.gpsimd.memset(tab_s[:, T // 2 :].bitcast(I32), 0)
        nc.vector.memset(w2s_raw[:].rearrange("p a c -> p (a c)").bitcast(I32), 0)
        nc.vector.memset(v_s[1][:].bitcast(I32), 0)
        ident = sb("ident", [P, P], F32)
        make_identity(nc, ident[:])

        tab_w = [sb("tab_w0", [P, T], U32), shared("tab_w1", [P, T], U32, AT_TAB_W1)]
        w2w_raw = sb("w2w_raw", [P, PASSES, 2 * H], U8)

        def load_table(a, cols):
            words = tab_words[a].rearrange("p t i -> p (t i)").bitcast(I32)
            nc.sync.dma_start(tab_w[a][:, cols].bitcast(I32), words[:, cols])

        load_table(0, slice(0, T // 4))
        offs_t = load_list("offs_t", offs)
        pos2_t = load_list("pos2_t", pos2)
        pos1_t = load_list("pos1_t", pos1)
        pos3_t = load_list("pos3_t", pos3)
        pos4_t = load_list("pos4_t", pos4)
        gam_t = sb("gam_t", [P, PACK], F32)
        nc.sync.dma_start(gam_t[:], gam.rearrange("(p t) -> p t", t=PACK))
        load_table(0, slice(T // 4, 5 * T // 8))
        for r in range(ROWS):
            nc.sync.dma_start(
                tab_s[r : P : QUAD // PASSES, :].bitcast(I32),
                tab_scales[:, r : ROWS * ROWS : ROWS, :].rearrange("a q c -> q a c").bitcast(I32),
            )
        load_table(0, slice(5 * T // 8, T))
        nc.sync.dma_start(w2w_raw[:].bitcast(I32), w2_words.rearrange("a p c -> p a c").bitcast(I32))
        for r in range(ROWS):
            nc.sync.dma_start(
                w2s_raw[r:P:QUAD, :, :].bitcast(I32),
                w2_scales[:, r : ROWS * ROWS : ROWS, :].rearrange("a q c -> q a c").bitcast(I32),
            )
        load_table(1, slice(0, T))

        v_w = {}

        def gather_words(a):
            cols = BANK // ENTRIES
            for hf in range(HALVES):
                v_w[a, hf] = sb(f"v_w{a}{hf}", [P, BANK], U32)
                nc.vector.tensor_copy(v_w[a, hf][:], tab_w[a][:].indirect(offs_t[:, hf * cols : (hf + 1) * cols]))

        raw = {}

        def load_weight(name, w, a, kib):
            raw[name, a] = shared(f"{name}_raw{a}", [P, PACK, H], F32, kib)
            nc.sync.dma_start(
                raw[name, a][:], w[a * K_PASS : (a + 1) * K_PASS, :].rearrange("(p j) c -> p j c", j=PACK)
            )

        nc.vector.tensor_copy(v_s[0][:], tab_s[:].indirect(offs_t[:]))
        for r in range(ROWS):
            nc.sync.dma_start(v_s[1][r:P:QUAD, :].bitcast(I32), v_s[0][QUAD // PASSES + r : P : QUAD, :].bitcast(I32))
        for a in range(PASSES):
            load_weight("w1", w1, a, AT_W1[a])
        gather_words(0)

        w2_w = sb("w2_w", [P, PASSES, 2 * H], U8)
        w2_s = sb("w2_s", [P, PASSES, H], U8)
        nc.scalar.copy(
            w2_w[:].bitcast(U16).rearrange("p a (t m) -> p a t m", t=PACK),
            w2w_raw[:].bitcast(U16).rearrange("p a (m t) -> p a t m", t=PACK),
        )
        nc.vector.tensor_copy(
            w2_s[:].rearrange("p a (t m) -> p a t m", t=PACK),
            w2s_raw[:].rearrange("p a (m t) -> p a t m", t=PACK),
        )
        gather_words(1)
        for a in range(PASSES):
            load_weight("w3", w3, a, AT_W3[a])

        def product(acc, a, t, hf, weight, weight_scale):
            if t < DIRECT:
                nc.tensor.matmul_mx(
                    out=acc[:], lhsT=weight, lhsT_scale=weight_scale,
                    rhs=v_w[a, hf][:].bitcast(E4M3X4), rhs_scale=v_s[a][:, hf * BANK : (hf + 1) * BANK],
                    start=(a == 0), stop=(a == PASSES - 1),
                )
                return
            for i in range(BLOCKS):
                first = hf * BANK + P * i
                nc.tensor.matmul_mx(
                    out=acc[:, P * i : P * (i + 1)], lhsT=v_w[a, hf][:, P * i : P * (i + 1)].bitcast(E4M3X4),
                    lhsT_scale=v_s[a][:, first : first + P], rhs=weight, rhs_scale=weight_scale,
                    start=(a, i) == (0, 0), stop=(a, i) == (PASSES - 1, BLOCKS - 1),
                )

        second = [sb(f"second{t}", [P, S], F32) for t in range(PACK)]
        accs = {}
        for hf in range(HALVES):
            for a in range(PASSES):
                for t in range(PACK):
                    if a == 0:
                        accs[t, hf] = psum.tile([P, BANK], F32, name="acc")
                    product(accs[t, hf], a, t, hf, w2_w[:, a, 2 * P * t : 2 * P * (t + 1)].bitcast(E2M1X4),
                            w2_s[:, a, P * t : P * (t + 1)])
                    if a == PASSES - 1:
                        nc.scalar.copy(second[t][:, hf * BANK : (hf + 1) * BANK], accs[t, hf][:])

        codes, scales = {}, {}

        def quantise_weight(name, a, copy, pieces):
            rounded = sb(f"{name}_bf{a}", [P, PACK * H], BF16)
            copy(
                rounded[:].rearrange("p (t m j) -> p m t j", t=PACK, j=PACK),
                raw[name, a][:].rearrange("p j (m t) -> p m t j", t=PACK),
            )
            codes[name, a] = sb(f"{name}_c{a}", [P, H], U32)
            scales[name, a] = sb(f"{name}_s{a}", [P, H], U8)
            step = H // pieces
            for first in range(0, H, step):
                nc.vector.quantize_mx(
                    out=codes[name, a][:, first : first + step].bitcast(E4M3X4),
                    scales=scales[name, a][:, first : first + step],
                    in_=rounded[:, PACK * first : PACK * (first + step)],
                )

        def float_product(name, t, hf):
            acc = psum.tile([P, BANK], F32, name="acc")
            for a in range(PASSES):
                product(acc, a, t, hf, codes[name, a][:, P * t : P * (t + 1)].bitcast(E4M3X4),
                        scales[name, a][:, P * t : P * (t + 1)])
            return acc

        for a in range(PASSES):
            quantise_weight("w1", a, nc.vector.tensor_copy, 1)
        gm_t = shared("gm_t", [P, PACK, KEPT], F32, AT_GM)
        nc.sync.dma_start(gm_t[:], gm.rearrange("(p t) j -> p t j", t=PACK))
        w4_w = shared("w4_w", [P, 2 * N], U8, AT_W4_W)
        nc.sync.dma_start(w4_w[:].bitcast(I32), w4_words[0].bitcast(I32))
        w4_s = shared("w4_s", [P, N], U8, AT_W4_S)
        nc.gpsimd.memset(w4_s[:].bitcast(I32), 0)
        for r in range(ROWS):
            nc.sync.dma_start(w4_s[r:P:QUAD, :].bitcast(I32), w4_scales[0, r : ROWS * ROWS : ROWS, :].bitcast(I32))
        quantise_weight("w3", 0, nc.scalar.copy, 1)
        quantise_weight("w3", 1, nc.scalar.copy, 2)

        larger = [sb(f"larger{t}", [P, S], F32) for t in range(PACK)]
        for t in range(PACK):
            for hf in range(HALVES):
                cols = slice(hf * BANK, (hf + 1) * BANK)
                acc = float_product("w1", t, hf)
                nc.vector.tensor_tensor(larger[t][:, cols], acc[:], second[t][:, cols], ALU.max)

        h = [sb(f"h{t}", [P, S], F32) for t in range(PACK)]
        picked = [sb(f"picked{t}", [P, PAIRS], F32) for t in range(PACK)]
        gate = [sb(f"gate{t}", [P, PAIRS], F32) for t in range(PACK)]
        a1 = [sb(f"a1_{t}", [P, PAIRS], F32) for t in range(PACK)]
        kept = [sb(f"kept{t}", [P, KEPT], F32) for t in range(PACK)]
        a2 = sb("a2", [P, PACK, KEPT], F32)

        def features(t):
            for hf in range(HALVES):
                cols = slice(hf * BANK, (hf + 1) * BANK)
                acc = float_product("w3", t, hf)
                if t < DIRECT:
                    nc.vector.tensor_tensor(h[t][:, cols], acc[:], larger[t][:, cols], ALU.add)
                    continue
                third = sb(f"third{t}{hf}", [P, BANK], F32)
                nc.scalar.copy(third[:], acc[:])
                turned = psum.tile([P, BANK], F32, name="turned", bufs=TURN_BANKS)
                for n, term in enumerate((larger[t][:, cols], third[:])):
                    for i in range(BLOCKS):
                        nc.tensor.matmul(
                            turned[:, P * i : P * (i + 1)], lhsT=term[:, P * i : P * (i + 1)], rhs=ident[:],
                            is_transpose=True, start=(n, i) == (0, 0), stop=(n, i) == (1, BLOCKS - 1),
                        )
                nc.scalar.copy(h[t][:, cols], turned[:])

        def pick_second(t):
            nc.vector.tensor_copy(picked[t][:], h[t][:].indirect(pos2_t[:]))
            nc.scalar.activation(gate[t][:], picked[t][:], ACT.Tanh, scale=gam_t[:, t : t + 1])

        def pair(t):
            nc.vector.tensor_tensor(a1[t][:], h[t][:].indirect(pos1_t[:]), gate[t][:], ALU.mult)

        def keep_pairs(t, first, end):
            entries = pos3_t[:, first // ENTRIES : end // ENTRIES]
            nc.vector.tensor_tensor(kept[t][:, first:end], a1[t][:].indirect(entries), gm_t[:, t, first:end], ALU.mult)

        def add_deed(t, first, end):
            entries = pos4_t[:, first // ENTRIES : end // ENTRIES]
            nc.vector.tensor_tensor(a2[:, t, first:end], h[t][:].indirect(entries), kept[t][:, first:end], ALU.add)

        features(0)
        pick_second(0)
        for t in range(1, PACK):
            features(t)
        last = PACK - 1
        for t in range(last):
            pair(t)
            pick_second(t + 1)
            keep_pairs(t, 0, KEPT)
            if t > 0:
                add_deed(t - 1, 0, KEPT)
        pair(last)

        a2_bf = [sb(f"a2_bf{u}", [P, PART * PACK], BF16) for u in range(KEPT // PART)]

        def round_a2(u):
            nc.vector.tensor_copy(
                a2_bf[u][:].rearrange("p (c i t) -> p c t i", i=4, t=PACK),
                a2[:, :, PART * u : PART * (u + 1)].rearrange("p t (c i) -> p c t i", i=4),
            )

        def score(u, copies):
            a2_c = sb(f"a2_c{u}", [P, PART], U32)
            a2_s = sb(f"a2_s{u}", [P, PART], U8)
            nc.vector.quantize_mx(out=a2_c[:].bitcast(E4M3X4), scales=a2_s[:], in_=a2_bf[u][:])
            groups = N // P // len(copies)
            for g, copy in enumerate(copies):
                acc = psum.tile([P, groups, PART], F32, name="acc")
                for i in range(groups):
                    c = g * groups + i
                    nc.tensor.matmul_mx(
                        out=acc[:, i, :], lhsT=w4_w[:, 2 * P * c : 2 * P * (c + 1)].bitcast(E2M1X4),
                        lhsT_scale=w4_s[:, P * c : P * (c + 1)],
                        rhs=a2_c[:].bitcast(E4M3X4), rhs_scale=a2_s[:], start=True, stop=True,
                    )
                result = sb(f"result{u}{g}", [P, groups, PART], F32)
                copy(result[:], acc[:])
                rows = out[g * groups * P : (g + 1) * groups * P, PART * u : PART * (u + 1)]
                nc.sync.dma_start(rows.rearrange("(i p) j -> p i j", p=P), result[:])

        keep_pairs(last, 0, PART)
        add_deed(last - 1, 0, KEPT)
        add_deed(last, 0, PART)
        keep_pairs(last, PART, KEPT)
        round_a2(0)
        add_deed(last, PART, KEPT)
        score(0, [nc.scalar.copy, nc.scalar.copy])
        round_a2(1)
        score(1, [nc.scalar.copy, nc.vector.tensor_copy])
